import numpy as np
import ml_dtypes


def mxq(x, axis, fmt="e4m3"):
    dtype, down = {"e4m3": (ml_dtypes.float8_e4m3fn, 7), "e5m2": (ml_dtypes.float8_e5m2, 14)}[fmt]
    v = np.moveaxis(np.asarray(x, np.float32).astype(ml_dtypes.bfloat16).astype(np.float64), axis, -1)
    blocks = v.reshape(v.shape[:-1] + (-1, 32))
    amax = np.abs(blocks).max(-1, keepdims=True)
    byte = np.maximum(np.where(amax > 0, np.frexp(amax)[1] - 1 + 127, 0) - down, 1)
    scale = np.exp2(byte - 127.0)
    codes = (blocks / scale).astype(np.float32).astype(dtype).astype(np.float64)
    return np.moveaxis((codes * scale).reshape(v.shape), -1, axis)


WIDE = False


def mx_kscale(k):
    if not WIDE:
        return np.ones(k)
    levels = np.array([10, -10, 5, -5, 0])
    if k % 512:
        return np.exp2(np.random.permutation(np.resize(levels, k // 32))).repeat(32)
    a = np.empty((k // 512, 16))
    for p in range(k // 512):
        a[p, :8] = np.random.permutation(np.resize(levels, 8))
        for g in range(8):
            far = levels[np.abs(levels - a[p, g]) >= 10]
            a[p, g + 8] = far[np.random.randint(len(far))]
    return np.exp2(a.ravel()).repeat(32)


def f64(x):
    return np.asarray(x).astype(np.float64)


def striped(idx):
    return np.tile(np.asarray(idx).reshape(-1, 16).T, (8, 1)).astype(np.uint16)


def unstriped(offs):
    return offs[:16].T.reshape(-1).astype(np.int64)


E2M1 = np.array([0.0, 0.5, 1.0, 1.5, 2.0, 3.0, 4.0, 6.0, -0.0, -0.5, -1.0, -1.5, -2.0, -3.0, -4.0, -6.0])


def pack_weight(w, fmt):
    k, n = w.shape
    w = f64(np.asarray(w, np.float32).astype(ml_dtypes.bfloat16)).reshape(k // 32, 32, n)
    amax = np.abs(w).max(1)
    if fmt == "e4m3":
        byte = np.frexp(amax)[1] - 1 + 127 - 7
    else:
        mant, ex = np.frexp(amax / 6.0)
        byte = np.where(mant > 0.5, ex, ex - 1) + 127
    byte = np.clip(np.where(amax > 0, byte, 1), 1, 254)
    scaled = (w * np.exp2(127.0 - byte)[:, None, :]).reshape(k, n).astype(np.float32)
    by_word = np.ascontiguousarray(scaled.reshape(k // 512, 128, 4, n).transpose(0, 1, 3, 2))
    if fmt == "e4m3":
        words = by_word.astype(ml_dtypes.float8_e4m3fn).view(np.uint8)
    else:
        c = by_word.astype(ml_dtypes.float4_e2m1fn).view(np.uint8) & 0xF
        words = (c[..., 0::2] | (c[..., 1::2] << 4)).reshape(k // 512, 128, 2 * n)
    return np.ascontiguousarray(words), np.ascontiguousarray(byte.astype(np.uint8).reshape(k // 512, 16, n))


def unpack_weight(words, scales, fmt):
    g, _, n = scales.shape
    words = np.ascontiguousarray(words).reshape(g, 128, n, -1)
    if fmt == "e4m3":
        vals = words.view(ml_dtypes.float8_e4m3fn).astype(np.float64)
    else:
        nib = np.empty((g, 128, n, 4), np.uint8)
        nib[..., 0::2] = words & 0xF
        nib[..., 1::2] = words >> 4
        vals = E2M1[nib]
    vals = vals * np.repeat(np.exp2(scales.astype(np.float64) - 127.0), 8, axis=1)[..., None]
    return vals.transpose(0, 1, 3, 2).reshape(g * 512, n)


D, T, V, I, Q = 512, 4096, 2048, 512, 128


def setup_inputs():
    n = np.random.standard_normal
    idx = np.random.permutation(T)[:V]
    idx2 = np.random.permutation(V)[:I]
    idx3 = np.random.permutation(V)[:I]
    fd = mx_kscale(D)
    vocp = pack_weight(n((D, T)) / fd[:, None], "e4m3")
    return {
        "ht": (n((D, Q)) * 1.0 / np.sqrt(D) * fd[:, None]).astype(np.float32),
        "voc_words": vocp[0],
        "voc_scales": vocp[1],
        "da": (np.random.uniform(0.0, 0.0008, (Q, I))).astype(np.float32),
        "db": (np.random.uniform(0.0, 0.0008, (Q, I))).astype(np.float32),
        "offs": striped(idx),
        "offs2": striped(idx2),
        "offs3": striped(idx3),
    }


def reference(ht, voc_words, voc_scales, da, db, offs, offs2, offs3):
    idx = unstriped(offs)
    idx2 = unstriped(offs2)
    idx3 = unstriped(offs3)
    vocu = unpack_weight(voc_words, voc_scales, "e4m3")
    htq = mxq(f64(ht), 0, "e4m3")
    vocidxg = vocu[:, idx]
    a = htq.T @ vocidxg
    p = np.exp(a - np.max(a, axis=1, keepdims=True))
    fa = np.zeros((Q, V))
    fa[:, idx2] = f64(da)
    u1 = np.maximum(p / np.sum(p, axis=1, keepdims=True) - fa, 0.0)
    fb = np.zeros((Q, V))
    fb[:, idx3] = f64(db)
    u2 = np.maximum(u1 / np.sum(u1, axis=1, keepdims=True) - fb, 0.0)
    y = u2 / np.sum(u2, axis=1, keepdims=True) * 2048.0
    return y

@@ -1,0 +1,119 @@
+from contextlib import ExitStack
+
+import concourse.mybir as mybir
+
+F32 = mybir.dt.float32
+BF16 = mybir.dt.bfloat16
+I32 = mybir.dt.int32
+U32 = mybir.dt.uint32
+U16 = mybir.dt.uint16
+U8 = mybir.dt.uint8
+FP8X4 = mybir.dt.float8_e4m3fn_x4
+ALU = mybir.AluOpType
+ACT = mybir.ActivationFunctionType
+AX = mybir.AxisListType
+
+P = 128
+D, T, V, I, Q = 512, 4096, 2048, 512, 128
+PACK = 4
+BANK = 512
+NB = V // BANK
+GW = 1024
+CH = 256
+NCH = V // CH
+FLOPS = 2 * D * V * Q
+
+
+def tile_attend_twodrafts_kernel(tc, ht, voc_words, voc_scales, da, db, offs, offs2, offs3, out):
+    nc = tc.nc
+    with ExitStack() as ctx:
+        keep = ctx.enter_context(tc.tile_pool(name="keep", bufs=1))
+        psum = ctx.enter_context(tc.psum_pool(name="psum", bufs=1))
+
+        l1 = keep.tile([P, V // 16], U16, name="l1")
+        l2 = keep.tile([P, I // 16], U16, name="l2")
+        l3 = keep.tile([P, I // 16], U16, name="l3")
+        words = keep.tile([P, T], I32, name="words", align_bytes=64)
+        scales = keep.tile([P, T], U8, name="scales", align_bytes=64)
+        da_sb = keep.tile([P, I], F32, name="da_sb")
+        db_sb = keep.tile([P, I], F32, name="db_sb")
+        nda = keep.tile([P, I], F32, name="nda")
+        fa = keep.tile([P, V], F32, name="fa")
+        fb = keep.tile([P, V], F32, name="fb")
+        h_raw = keep.tile([P, PACK, Q], F32, name="h_raw")
+        h_bf = keep.tile([P, Q, PACK], BF16, name="h_bf", align_bytes=64)
+        h_codes = keep.tile([P, Q], U32, name="h_codes", align_bytes=64)
+        h_scales = keep.tile([P, Q], U8, name="h_scales", align_bytes=64)
+        g_words = keep.tile([P, V], U32, name="g_words", align_bytes=64)
+        g_scales = keep.tile([P, V], U8, name="g_scales", align_bytes=64)
+        warm2 = keep.tile([P, 1], F32, name="warm2")
+
+        nc.vector.memset(scales[:].bitcast(I32), 0)
+        nc.vector.memset(fb[:], 0.0)
+        nc.vector.memset(fa[:], 0.0)
+
+        nc.sync.dma_start(l3[:], offs3)
+        nc.sync.dma_start(db_sb[:], db)
+        nc.sync.dma_start(l1[:], offs)
+        for quad in range(4):
+            nc.scalar.dma_start(scales[32 * quad : 32 * quad + 4, :].bitcast(I32),
+                                voc_scales[0, 4 * quad : 4 * quad + 4, :].bitcast(I32))
+        nc.sync.dma_start(h_raw[:], ht.rearrange("(p j) q -> p j q", j=PACK))
+        nc.sync.dma_start(words[:], voc_words[0].rearrange("p n t -> p (n t)").bitcast(I32))
+        nc.sync.dma_start(l2[:], offs2)
+        nc.sync.dma_start(da_sb[:], da)
+
+        nc.scalar.activation(warm2[:], db_sb[:, 0:1], ACT.Exp)
+        nc.vector.tensor_copy(fb[:].indirect(l3[:]), db_sb[:])
+        nc.scalar.copy(h_bf[:], h_raw[:].rearrange("p j q -> p q j"))
+        nc.vector.tensor_copy(g_scales[:], scales[:].indirect(l1[:]))
+        nc.vector.quantize_mx(out=h_codes[:].bitcast(FP8X4), scales=h_scales[:],
+                              in_=h_bf[:].rearrange("p q j -> p (q j)"))
+        nc.scalar.activation(nda[:], da_sb[:], ACT.Copy, scale=-1.0)
+
+        for g in range(V // GW):
+            nc.vector.tensor_copy(g_words[:, g * GW : (g + 1) * GW],
+                                  words[:].bitcast(U32).indirect(l1[:, g * GW // 16 : (g + 1) * GW // 16]))
+        banks = [psum.tile([P, BANK], F32, name=f"bank{b}") for b in range(NB)]
+        bank_max = keep.tile([P, NB], F32, name="bank_max")
+        for b in range(NB):
+            cols = slice(b * BANK, (b + 1) * BANK)
+            nc.tensor.matmul_mx(out=banks[b][:], lhsT=h_codes[:].bitcast(FP8X4), lhsT_scale=h_scales[:],
+                                rhs=g_words[:, cols].bitcast(FP8X4), rhs_scale=g_scales[:, cols],
+                                start=True, stop=True)
+            nc.vector.tensor_reduce(bank_max[:, b : b + 1], banks[b][:], AX.X, ALU.max)
+        neg_max = keep.tile([P, 1], F32, name="neg_max")
+        nc.vector.tensor_reduce(neg_max[:], bank_max[:], AX.X, ALU.max, negate=True)
+        nc.vector.tensor_copy(fa[:].indirect(l2[:]), nda[:])
+
+        p = keep.tile([P, V], F32, name="p")
+        p_part = keep.tile([P, NB], F32, name="p_part")
+        p_part2 = keep.tile([P, NB], F32, name="p_part2")
+        p_sum = keep.tile([P, 1], F32, name="p_sum")
+        for b in range(NB):
+            nc.scalar.activation(p[:, b * BANK : (b + 1) * BANK], banks[b][:], ACT.Exp, bias=neg_max[:],
+                                 accum_out=p_part[:, b : b + 1])
+        nc.scalar.activation(p_part2[:], p_part[:], ACT.Copy, accum_out=p_sum[:])
+
+        def take_off(name, cur, draft, factor, sum_op):
+            t = keep.tile([P, V + NCH], F32, name=name + "_t")
+            u = keep.tile([P, V + NCH], F32, name=name + "_u")
+            total = keep.tile([P, 1], F32, name=name + "_s")
+            for c in range(NCH):
+                cols = slice(c * CH, (c + 1) * CH)
+                nc.vector.scalar_tensor_tensor(t[:, cols], draft[:, cols], factor[:], cur[:, cols], ALU.mult, ALU.add)
+                if c < NCH - 1:
+                    nc.scalar.activation(u[:, cols], t[:, cols], ACT.Relu, accum_out=t[:, V + c : V + c + 1])
+            last = slice(V - CH, V + NCH - 1)
+            nc.vector.tensor_scalar(u[:, last], t[:, last], 0.0, None, ALU.max, sum_op, accum_out=total[:])
+            return u, total
+
+        u1, neg_s1 = take_off("one", p, fa, p_sum, ALU.subtract)
+        u2, s2 = take_off("two", u1, fb, neg_s1, ALU.add)
+        rec = keep.tile([P, 1], F32, name="rec")
+        nc.vector.reciprocal(rec[:], s2[:])
+        y = keep.tile([P, V], F32, name="y")
+        for b in range(NB):
+            cols = slice(b * BANK, (b + 1) * BANK)
+            nc.vector.tensor_scalar(y[:, cols], u2[:, cols], rec[:], float(V), ALU.mult, ALU.mult)
+            (nc.sync if b % 2 == 0 else nc.scalar).dma_start(out[:, cols], y[:, cols])

@@ -18,10 +18,17 @@ D, T, V, I, Q = 512, 4096, 2048, 512, 128
 PACK = 4
 BANK = 512
 NB = V // BANK
-GW = 1024
-CH = 256
-NCH = V // CH
+HALF = I // 2
+GATHERS = (1024, 512, 512)
+FIRST_CHUNKS = (256, 384, 384, 512, 512)
+SECOND_CHUNKS = (128, 192, 256, 320, 320, 384)
+STORES = (256, 512, 640, 640)
 FLOPS = 2 * D * V * Q
+
+
+def runs(widths):
+    starts = [sum(widths[:n]) for n in range(len(widths))]
+    return [slice(s, s + w) for s, w in zip(starts, widths)]
 
 
 def tile_attend_twodrafts_kernel(tc, ht, voc_words, voc_scales, da, db, offs, offs2, offs3, out):
@@ -33,87 +40,99 @@ def tile_attend_twodrafts_kernel(tc, ht, voc_words, voc_scales, da, db, offs, of
         l1 = keep.tile([P, V // 16], U16, name="l1")
         l2 = keep.tile([P, I // 16], U16, name="l2")
         l3 = keep.tile([P, I // 16], U16, name="l3")
-        words = keep.tile([P, T], I32, name="words", align_bytes=64)
+        warm_in = keep.tile([P, 1], F32, name="warm_in", tag="words", align_bytes=64)
         scales = keep.tile([P, T], U8, name="scales", align_bytes=64)
-        da_sb = keep.tile([P, I], F32, name="da_sb")
-        db_sb = keep.tile([P, I], F32, name="db_sb")
-        nda = keep.tile([P, I], F32, name="nda")
-        fa = keep.tile([P, V], F32, name="fa")
+        db_lo = keep.tile([P, HALF], F32, name="db_lo", tag="fa")
         fb = keep.tile([P, V], F32, name="fb")
         h_raw = keep.tile([P, PACK, Q], F32, name="h_raw")
         h_bf = keep.tile([P, Q, PACK], BF16, name="h_bf", align_bytes=64)
         h_codes = keep.tile([P, Q], U32, name="h_codes", align_bytes=64)
         h_scales = keep.tile([P, Q], U8, name="h_scales", align_bytes=64)
-        g_words = keep.tile([P, V], U32, name="g_words", align_bytes=64)
         g_scales = keep.tile([P, V], U8, name="g_scales", align_bytes=64)
-        warm2 = keep.tile([P, 1], F32, name="warm2")
+        warm = keep.tile([P, 1], F32, name="warm")
 
         nc.vector.memset(scales[:].bitcast(I32), 0)
         nc.vector.memset(fb[:], 0.0)
-        nc.vector.memset(fa[:], 0.0)
+        nc.gpsimd.memset(warm_in[:], 0.0)
+        nc.scalar.activation(warm[:], warm_in[:], ACT.Exp)
 
         nc.sync.dma_start(l3[:], offs3)
-        nc.sync.dma_start(db_sb[:], db)
+        nc.sync.dma_start(db_lo[:], db[:, 0:HALF])
         nc.sync.dma_start(l1[:], offs)
         for quad in range(4):
-            nc.scalar.dma_start(scales[32 * quad : 32 * quad + 4, :].bitcast(I32),
+            nc.sync.dma_start(scales[32 * quad : 32 * quad + 4, :].bitcast(I32),
                                 voc_scales[0, 4 * quad : 4 * quad + 4, :].bitcast(I32))
         nc.sync.dma_start(h_raw[:], ht.rearrange("(p j) q -> p j q", j=PACK))
-        nc.sync.dma_start(words[:], voc_words[0].rearrange("p n t -> p (n t)").bitcast(I32))
         nc.sync.dma_start(l2[:], offs2)
-        nc.sync.dma_start(da_sb[:], da)
+        words = keep.tile([P, T], I32, name="words", tag="words", align_bytes=64)
+        nc.sync.dma_start(words[:], voc_words[0].rearrange("p n t -> p (n t)").bitcast(I32))
 
-        nc.scalar.activation(warm2[:], db_sb[:, 0:1], ACT.Exp)
-        nc.vector.tensor_copy(fb[:].indirect(l3[:]), db_sb[:])
+        nc.vector.tensor_copy(fb[:].indirect(l3[:, 0 : HALF // 16]), db_lo[:])
+        fa = keep.tile([P, V], F32, name="fa", tag="fa")
+        nc.gpsimd.memset(fa[:], 0.0)
         nc.scalar.copy(h_bf[:], h_raw[:].rearrange("p j q -> p q j"))
         nc.vector.tensor_copy(g_scales[:], scales[:].indirect(l1[:]))
         nc.vector.quantize_mx(out=h_codes[:].bitcast(FP8X4), scales=h_scales[:],
                               in_=h_bf[:].rearrange("p q j -> p (q j)"))
-        nc.scalar.activation(nda[:], da_sb[:], ACT.Copy, scale=-1.0)
 
-        for g in range(V // GW):
-            nc.vector.tensor_copy(g_words[:, g * GW : (g + 1) * GW],
-                                  words[:].bitcast(U32).indirect(l1[:, g * GW // 16 : (g + 1) * GW // 16]))
+        g_words = []
+        for g, cols in enumerate(runs(GATHERS)):
+            gathered = keep.tile([P, GATHERS[g]], U32, name=f"g_words{g}", tag=f"g_words{g}", align_bytes=64)
+            nc.vector.tensor_copy(gathered[:],
+                                  words[:].bitcast(U32).indirect(l1[:, cols.start // 16 : cols.stop // 16]))
+            g_words.extend(gathered[:, s : s + BANK] for s in range(0, GATHERS[g], BANK))
         banks = [psum.tile([P, BANK], F32, name=f"bank{b}") for b in range(NB)]
         bank_max = keep.tile([P, NB], F32, name="bank_max")
         for b in range(NB):
             cols = slice(b * BANK, (b + 1) * BANK)
             nc.tensor.matmul_mx(out=banks[b][:], lhsT=h_codes[:].bitcast(FP8X4), lhsT_scale=h_scales[:],
-                                rhs=g_words[:, cols].bitcast(FP8X4), rhs_scale=g_scales[:, cols],
+                                rhs=g_words[b].bitcast(FP8X4), rhs_scale=g_scales[:, cols],
                                 start=True, stop=True)
             nc.vector.tensor_reduce(bank_max[:, b : b + 1], banks[b][:], AX.X, ALU.max)
-        neg_max = keep.tile([P, 1], F32, name="neg_max")
+        neg_max = keep.tile([P, 1], F32, name="neg_max", tag="neg_max")
         nc.vector.tensor_reduce(neg_max[:], bank_max[:], AX.X, ALU.max, negate=True)
-        nc.vector.tensor_copy(fa[:].indirect(l2[:]), nda[:])
+
+        da_sb = keep.tile([P, I], F32, name="da_sb", tag="g_words1", align_bytes=64)
+        nc.sync.dma_start(da_sb[:], da)
+        nc.vector.tensor_copy(fa[:].indirect(l2[:]), da_sb[:])
 
         p = keep.tile([P, V], F32, name="p")
         p_part = keep.tile([P, NB], F32, name="p_part")
-        p_part2 = keep.tile([P, NB], F32, name="p_part2")
-        p_sum = keep.tile([P, 1], F32, name="p_sum")
         for b in range(NB):
             nc.scalar.activation(p[:, b * BANK : (b + 1) * BANK], banks[b][:], ACT.Exp, bias=neg_max[:],
                                  accum_out=p_part[:, b : b + 1])
-        nc.scalar.activation(p_part2[:], p_part[:], ACT.Copy, accum_out=p_sum[:])
+        neg_part = keep.tile([P, NB], F32, name="neg_part")
+        neg_s0 = keep.tile([P, 1], F32, name="neg_s0")
+        nc.scalar.activation(neg_part[:], p_part[:], ACT.Copy, scale=-1.0, accum_out=neg_s0[:])
+        db_hi = keep.tile([P, HALF], F32, name="db_hi", tag="neg_max")
+        nc.sync.dma_start(db_hi[:], db[:, HALF:I])
 
-        def take_off(name, cur, draft, factor, sum_op):
-            t = keep.tile([P, V + NCH], F32, name=name + "_t")
-            u = keep.tile([P, V + NCH], F32, name=name + "_u")
-            total = keep.tile([P, 1], F32, name=name + "_s")
-            for c in range(NCH):
-                cols = slice(c * CH, (c + 1) * CH)
-                nc.vector.scalar_tensor_tensor(t[:, cols], draft[:, cols], factor[:], cur[:, cols], ALU.mult, ALU.add)
-                if c < NCH - 1:
-                    nc.scalar.activation(u[:, cols], t[:, cols], ACT.Relu, accum_out=t[:, V + c : V + c + 1])
-            last = slice(V - CH, V + NCH - 1)
-            nc.vector.tensor_scalar(u[:, last], t[:, last], 0.0, None, ALU.max, sum_op, accum_out=total[:])
-            return u, total
+        t1 = keep.tile([P, V], F32, name="t1")
+        u1 = keep.tile([P, V], F32, name="u1")
+        n1 = len(FIRST_CHUNKS)
+        u1_part = keep.tile([P, n1], F32, name="u1_part")
+        for c, cols in enumerate(runs(FIRST_CHUNKS)):
+            nc.vector.scalar_tensor_tensor(t1[:, cols], fa[:, cols], neg_s0[:], p[:, cols], ALU.mult, ALU.add)
+            nc.scalar.activation(u1[:, cols], t1[:, cols], ACT.Relu, accum_out=u1_part[:, c : c + 1])
+        neg_part1 = keep.tile([P, n1], F32, name="neg_part1")
+        neg_s1 = keep.tile([P, 1], F32, name="neg_s1")
+        nc.scalar.activation(neg_part1[:], u1_part[:], ACT.Copy, scale=-1.0, accum_out=neg_s1[:])
+        nc.vector.tensor_copy(fb[:].indirect(l3[:, HALF // 16 : I // 16]), db_hi[:])
 
-        u1, neg_s1 = take_off("one", p, fa, p_sum, ALU.subtract)
-        u2, s2 = take_off("two", u1, fb, neg_s1, ALU.add)
+        n2 = len(SECOND_CHUNKS)
+        t2 = keep.tile([P, V + n2], F32, name="t2")
+        u2 = keep.tile([P, V + n2], F32, name="u2")
+        for c, cols in enumerate(runs(SECOND_CHUNKS)):
+            nc.vector.scalar_tensor_tensor(t2[:, cols], fb[:, cols], neg_s1[:], u1[:, cols], ALU.mult, ALU.add)
+            nc.scalar.activation(u2[:, cols], t2[:, cols], ACT.Relu, accum_out=t2[:, V + c : V + c + 1])
+        own = sum(SECOND_CHUNKS)
+        nc.vector.scalar_tensor_tensor(t2[:, own:V], fb[:, own:V], neg_s1[:], u1[:, own:V], ALU.mult, ALU.add)
+        s2 = keep.tile([P, 1], F32, name="s2")
+        nc.vector.tensor_scalar(u2[:, own:], t2[:, own:], 0.0, None, ALU.max, ALU.add, accum_out=s2[:])
+
         rec = keep.tile([P, 1], F32, name="rec")
         nc.vector.reciprocal(rec[:], s2[:])
         y = keep.tile([P, V], F32, name="y")
-        for b in range(NB):
-            cols = slice(b * BANK, (b + 1) * BANK)
+        for n, cols in enumerate(runs(STORES)):
             nc.vector.tensor_scalar(y[:, cols], u2[:, cols], rec[:], float(V), ALU.mult, ALU.mult)
-            (nc.sync if b % 2 == 0 else nc.scalar).dma_start(out[:, cols], y[:, cols])
+            (nc.sync if n % 2 == 0 else nc.scalar).dma_start(out[:, cols], y[:, cols])

@@ -16,9 +16,13 @@ AX = mybir.AxisListType
 P = 128
 D, T, V, I, Q = 512, 4096, 2048, 512, 128
 PACK = 4
+LIST_COL = 16
+SCALE_ROWS = D // 32
+QUADRANT = 32
 BANK = 512
 NB = V // BANK
 HALF = I // 2
+
 GATHERS = (1024, 512, 512)
 FIRST_CHUNKS = (256, 384, 384, 512, 512)
 SECOND_CHUNKS = (128, 192, 256, 320, 320, 384)
@@ -37,19 +41,18 @@ def tile_attend_twodrafts_kernel(tc, ht, voc_words, voc_scales, da, db, offs, of
         keep = ctx.enter_context(tc.tile_pool(name="keep", bufs=1))
         psum = ctx.enter_context(tc.psum_pool(name="psum", bufs=1))
 
-        l1 = keep.tile([P, V // 16], U16, name="l1")
-        l2 = keep.tile([P, I // 16], U16, name="l2")
-        l3 = keep.tile([P, I // 16], U16, name="l3")
-        warm_in = keep.tile([P, 1], F32, name="warm_in", tag="words", align_bytes=64)
+        l1 = keep.tile([P, V // LIST_COL], U16, name="l1")
+        l2 = keep.tile([P, I // LIST_COL], U16, name="l2")
+        l3 = keep.tile([P, I // LIST_COL], U16, name="l3")
+        warm_in = keep.tile([P, 1], F32, name="warm_in", tag="g_words2", align_bytes=64)
         scales = keep.tile([P, T], U8, name="scales", align_bytes=64)
         db_lo = keep.tile([P, HALF], F32, name="db_lo", tag="fa")
         fb = keep.tile([P, V], F32, name="fb")
-        h_raw = keep.tile([P, PACK, Q], F32, name="h_raw")
-        h_bf = keep.tile([P, Q, PACK], BF16, name="h_bf", align_bytes=64)
+        h_bf = keep.tile([P, Q, PACK], BF16, name="h_bf", tag="g_words1", align_bytes=64)
         h_codes = keep.tile([P, Q], U32, name="h_codes", align_bytes=64)
         h_scales = keep.tile([P, Q], U8, name="h_scales", align_bytes=64)
         g_scales = keep.tile([P, V], U8, name="g_scales", align_bytes=64)
-        warm = keep.tile([P, 1], F32, name="warm")
+        warm = keep.tile([P, 1], F32, name="warm", tag="words", align_bytes=64)
 
         nc.vector.memset(scales[:].bitcast(I32), 0)
         nc.vector.memset(fb[:], 0.0)
@@ -57,17 +60,18 @@ def tile_attend_twodrafts_kernel(tc, ht, voc_words, voc_scales, da, db, offs, of
         nc.scalar.activation(warm[:], warm_in[:], ACT.Exp)
 
         nc.sync.dma_start(l3[:], offs3)
-        nc.sync.dma_start(db_lo[:], db[:, 0:HALF])
         nc.sync.dma_start(l1[:], offs)
-        for quad in range(4):
-            nc.sync.dma_start(scales[32 * quad : 32 * quad + 4, :].bitcast(I32),
-                                voc_scales[0, 4 * quad : 4 * quad + 4, :].bitcast(I32))
-        nc.sync.dma_start(h_raw[:], ht.rearrange("(p j) q -> p j q", j=PACK))
+        nc.sync.dma_start(db_lo[:], db[:, 0:HALF])
+        for row in range(PACK):
+            nc.sync.dma_start(scales[row:P:QUADRANT, :].bitcast(I32),
+                              voc_scales[0, row:SCALE_ROWS:PACK, :].bitcast(I32))
         nc.sync.dma_start(l2[:], offs2)
         words = keep.tile([P, T], I32, name="words", tag="words", align_bytes=64)
         nc.sync.dma_start(words[:], voc_words[0].rearrange("p n t -> p (n t)").bitcast(I32))
+        h_raw = keep.tile([P, PACK, Q], F32, name="h_raw", tag="g_words2", align_bytes=64)
+        nc.sync.dma_start(h_raw[:], ht.rearrange("(p j) q -> p j q", j=PACK))
 
-        nc.vector.tensor_copy(fb[:].indirect(l3[:, 0 : HALF // 16]), db_lo[:])
+        nc.vector.tensor_copy(fb[:].indirect(l3[:, 0 : HALF // LIST_COL]), db_lo[:])
         fa = keep.tile([P, V], F32, name="fa", tag="fa")
         nc.gpsimd.memset(fa[:], 0.0)
         nc.scalar.copy(h_bf[:], h_raw[:].rearrange("p j q -> p q j"))
@@ -78,9 +82,10 @@ def tile_attend_twodrafts_kernel(tc, ht, voc_words, voc_scales, da, db, offs, of
         g_words = []
         for g, cols in enumerate(runs(GATHERS)):
             gathered = keep.tile([P, GATHERS[g]], U32, name=f"g_words{g}", tag=f"g_words{g}", align_bytes=64)
-            nc.vector.tensor_copy(gathered[:],
-                                  words[:].bitcast(U32).indirect(l1[:, cols.start // 16 : cols.stop // 16]))
+            entries = l1[:, cols.start // LIST_COL : cols.stop // LIST_COL]
+            nc.vector.tensor_copy(gathered[:], words[:].bitcast(U32).indirect(entries))
             g_words.extend(gathered[:, s : s + BANK] for s in range(0, GATHERS[g], BANK))
+
         banks = [psum.tile([P, BANK], F32, name=f"bank{b}") for b in range(NB)]
         bank_max = keep.tile([P, NB], F32, name="bank_max")
         for b in range(NB):
@@ -92,7 +97,7 @@ def tile_attend_twodrafts_kernel(tc, ht, voc_words, voc_scales, da, db, offs, of
         neg_max = keep.tile([P, 1], F32, name="neg_max", tag="neg_max")
         nc.vector.tensor_reduce(neg_max[:], bank_max[:], AX.X, ALU.max, negate=True)
 
-        da_sb = keep.tile([P, I], F32, name="da_sb", tag="g_words1", align_bytes=64)
+        da_sb = keep.tile([P, I], F32, name="da_sb", tag="g_words0", align_bytes=64)
         nc.sync.dma_start(da_sb[:], da)
         nc.vector.tensor_copy(fa[:].indirect(l2[:]), da_sb[:])
 
@@ -117,7 +122,7 @@ def tile_attend_twodrafts_kernel(tc, ht, voc_words, voc_scales, da, db, offs, of
         neg_part1 = keep.tile([P, n1], F32, name="neg_part1")
         neg_s1 = keep.tile([P, 1], F32, name="neg_s1")
         nc.scalar.activation(neg_part1[:], u1_part[:], ACT.Copy, scale=-1.0, accum_out=neg_s1[:])
-        nc.vector.tensor_copy(fb[:].indirect(l3[:, HALF // 16 : I // 16]), db_hi[:])
+        nc.vector.tensor_copy(fb[:].indirect(l3[:, HALF // LIST_COL : I // LIST_COL]), db_hi[:])
 
         n2 = len(SECOND_CHUNKS)
         t2 = keep.tile([P, V + n2], F32, name="t2")

from contextlib import ExitStack

import concourse.mybir as mybir

F32 = mybir.dt.float32
BF16 = mybir.dt.bfloat16
I32 = mybir.dt.int32
U32 = mybir.dt.uint32
U16 = mybir.dt.uint16
U8 = mybir.dt.uint8
FP8X4 = mybir.dt.float8_e4m3fn_x4
ALU = mybir.AluOpType
ACT = mybir.ActivationFunctionType
AX = mybir.AxisListType

P = 128
D, T, V, I, Q = 512, 4096, 2048, 512, 128
PACK = 4
LIST_COL = 16
SCALE_ROWS = D // 32
QUADRANT = 32
BANK = 512
NB = V // BANK
HALF = I // 2

GATHERS = (1024, 512, 512)
FIRST_CHUNKS = (256, 384, 384, 512, 512)
SECOND_CHUNKS = (128, 192, 256, 320, 320, 384)
STORES = (256, 512, 640, 640)
FLOPS = 2 * D * V * Q


def runs(widths):
    starts = [sum(widths[:n]) for n in range(len(widths))]
    return [slice(s, s + w) for s, w in zip(starts, widths)]


def tile_attend_twodrafts_kernel(tc, ht, voc_words, voc_scales, da, db, offs, offs2, offs3, out):
    nc = tc.nc
    with ExitStack() as ctx:
        keep = ctx.enter_context(tc.tile_pool(name="keep", bufs=1))
        psum = ctx.enter_context(tc.psum_pool(name="psum", bufs=1))

        l1 = keep.tile([P, V // LIST_COL], U16, name="l1")
        l2 = keep.tile([P, I // LIST_COL], U16, name="l2")
        l3 = keep.tile([P, I // LIST_COL], U16, name="l3")
        warm_in = keep.tile([P, 1], F32, name="warm_in", tag="g_words2", align_bytes=64)
        scales = keep.tile([P, T], U8, name="scales", align_bytes=64)
        db_lo = keep.tile([P, HALF], F32, name="db_lo", tag="fa")
        fb = keep.tile([P, V], F32, name="fb")
        h_bf = keep.tile([P, Q, PACK], BF16, name="h_bf", tag="g_words1", align_bytes=64)
        h_codes = keep.tile([P, Q], U32, name="h_codes", align_bytes=64)
        h_scales = keep.tile([P, Q], U8, name="h_scales", align_bytes=64)
        g_scales = keep.tile([P, V], U8, name="g_scales", align_bytes=64)
        warm = keep.tile([P, 1], F32, name="warm", tag="words", align_bytes=64)

        nc.vector.memset(scales[:].bitcast(I32), 0)
        nc.vector.memset(fb[:], 0.0)
        nc.gpsimd.memset(warm_in[:], 0.0)
        nc.scalar.activation(warm[:], warm_in[:], ACT.Exp)

        nc.sync.dma_start(l3[:], offs3)
        nc.sync.dma_start(l1[:], offs)
        nc.sync.dma_start(db_lo[:], db[:, 0:HALF])
        for row in range(PACK):
            nc.sync.dma_start(scales[row:P:QUADRANT, :].bitcast(I32),
                              voc_scales[0, row:SCALE_ROWS:PACK, :].bitcast(I32))
        nc.sync.dma_start(l2[:], offs2)
        words = keep.tile([P, T], I32, name="words", tag="words", align_bytes=64)
        nc.sync.dma_start(words[:], voc_words[0].rearrange("p n t -> p (n t)").bitcast(I32))
        h_raw = keep.tile([P, PACK, Q], F32, name="h_raw", tag="g_words2", align_bytes=64)
        nc.sync.dma_start(h_raw[:], ht.rearrange("(p j) q -> p j q", j=PACK))

        nc.vector.tensor_copy(fb[:].indirect(l3[:, 0 : HALF // LIST_COL]), db_lo[:])
        fa = keep.tile([P, V], F32, name="fa", tag="fa")
        nc.gpsimd.memset(fa[:], 0.0)
        nc.scalar.copy(h_bf[:], h_raw[:].rearrange("p j q -> p q j"))
        nc.vector.tensor_copy(g_scales[:], scales[:].indirect(l1[:]))
        nc.vector.quantize_mx(out=h_codes[:].bitcast(FP8X4), scales=h_scales[:],
                              in_=h_bf[:].rearrange("p q j -> p (q j)"))

        g_words = []
        for g, cols in enumerate(runs(GATHERS)):
            gathered = keep.tile([P, GATHERS[g]], U32, name=f"g_words{g}", tag=f"g_words{g}", align_bytes=64)
            entries = l1[:, cols.start // LIST_COL : cols.stop // LIST_COL]
            nc.vector.tensor_copy(gathered[:], words[:].bitcast(U32).indirect(entries))
            g_words.extend(gathered[:, s : s + BANK] for s in range(0, GATHERS[g], BANK))

        banks = [psum.tile([P, BANK], F32, name=f"bank{b}") for b in range(NB)]
        bank_max = keep.tile([P, NB], F32, name="bank_max")
        for b in range(NB):
            cols = slice(b * BANK, (b + 1) * BANK)
            nc.tensor.matmul_mx(out=banks[b][:], lhsT=h_codes[:].bitcast(FP8X4), lhsT_scale=h_scales[:],
                                rhs=g_words[b].bitcast(FP8X4), rhs_scale=g_scales[:, cols],
                                start=True, stop=True)
            nc.vector.tensor_reduce(bank_max[:, b : b + 1], banks[b][:], AX.X, ALU.max)
        neg_max = keep.tile([P, 1], F32, name="neg_max", tag="neg_max")
        nc.vector.tensor_reduce(neg_max[:], bank_max[:], AX.X, ALU.max, negate=True)

        da_sb = keep.tile([P, I], F32, name="da_sb", tag="g_words0", align_bytes=64)
        nc.sync.dma_start(da_sb[:], da)
        nc.vector.tensor_copy(fa[:].indirect(l2[:]), da_sb[:])

        p = keep.tile([P, V], F32, name="p")
        p_part = keep.tile([P, NB], F32, name="p_part")
        for b in range(NB):
            nc.scalar.activation(p[:, b * BANK : (b + 1) * BANK], banks[b][:], ACT.Exp, bias=neg_max[:],
                                 accum_out=p_part[:, b : b + 1])
        neg_part = keep.tile([P, NB], F32, name="neg_part")
        neg_s0 = keep.tile([P, 1], F32, name="neg_s0")
        nc.scalar.activation(neg_part[:], p_part[:], ACT.Copy, scale=-1.0, accum_out=neg_s0[:])
        db_hi = keep.tile([P, HALF], F32, name="db_hi", tag="neg_max")
        nc.sync.dma_start(db_hi[:], db[:, HALF:I])

        t1 = keep.tile([P, V], F32, name="t1")
        u1 = keep.tile([P, V], F32, name="u1")
        n1 = len(FIRST_CHUNKS)
        u1_part = keep.tile([P, n1], F32, name="u1_part")
        for c, cols in enumerate(runs(FIRST_CHUNKS)):
            nc.vector.scalar_tensor_tensor(t1[:, cols], fa[:, cols], neg_s0[:], p[:, cols], ALU.mult, ALU.add)
            nc.scalar.activation(u1[:, cols], t1[:, cols], ACT.Relu, accum_out=u1_part[:, c : c + 1])
        neg_part1 = keep.tile([P, n1], F32, name="neg_part1")
        neg_s1 = keep.tile([P, 1], F32, name="neg_s1")
        nc.scalar.activation(neg_part1[:], u1_part[:], ACT.Copy, scale=-1.0, accum_out=neg_s1[:])
        nc.vector.tensor_copy(fb[:].indirect(l3[:, HALF // LIST_COL : I // LIST_COL]), db_hi[:])

        n2 = len(SECOND_CHUNKS)
        t2 = keep.tile([P, V + n2], F32, name="t2")
        u2 = keep.tile([P, V + n2], F32, name="u2")
        for c, cols in enumerate(runs(SECOND_CHUNKS)):
            nc.vector.scalar_tensor_tensor(t2[:, cols], fb[:, cols], neg_s1[:], u1[:, cols], ALU.mult, ALU.add)
            nc.scalar.activation(u2[:, cols], t2[:, cols], ACT.Relu, accum_out=t2[:, V + c : V + c + 1])
        own = sum(SECOND_CHUNKS)
        nc.vector.scalar_tensor_tensor(t2[:, own:V], fb[:, own:V], neg_s1[:], u1[:, own:V], ALU.mult, ALU.add)
        s2 = keep.tile([P, 1], F32, name="s2")
        nc.vector.tensor_scalar(u2[:, own:], t2[:, own:], 0.0, None, ALU.max, ALU.add, accum_out=s2[:])

        rec = keep.tile([P, 1], F32, name="rec")
        nc.vector.reciprocal(rec[:], s2[:])
        y = keep.tile([P, V], F32, name="y")
        for n, cols in enumerate(runs(STORES)):
            nc.vector.tensor_scalar(y[:, cols], u2[:, cols], rec[:], float(V), ALU.mult, ALU.mult)
            (nc.sync if n % 2 == 0 else nc.scalar).dma_start(out[:, cols], y[:, cols])
